import numpy as np
import ml_dtypes


def mxq(x, axis, fmt="e4m3"):
    dtype, down = {"e4m3": (ml_dtypes.float8_e4m3fn, 7), "e5m2": (ml_dtypes.float8_e5m2, 14)}[fmt]
    v = np.moveaxis(np.asarray(x, np.float32).astype(ml_dtypes.bfloat16).astype(np.float64), axis, -1)
    blocks = v.reshape(v.shape[:-1] + (-1, 32))
    amax = np.abs(blocks).max(-1, keepdims=True)
    byte = np.maximum(np.where(amax > 0, np.frexp(amax)[1] - 1 + 127, 0) - down, 1)
    scale = np.exp2(byte - 127.0)
    codes = (blocks / scale).astype(np.float32).astype(dtype).astype(np.float64)
    return np.moveaxis((codes * scale).reshape(v.shape), -1, axis)


WIDE = False


def mx_kscale(k):
    if not WIDE:
        return np.ones(k)
    levels = np.array([30, -30])
    if k % 512:
        return np.exp2(np.random.permutation(np.resize(levels, k // 32))).repeat(32)
    a = np.empty((k // 512, 16))
    for p in range(k // 512):
        a[p, :8] = np.random.permutation(np.resize(levels, 8))
        for g in range(8):
            far = levels[np.abs(levels - a[p, g]) >= 10]
            a[p, g + 8] = far[np.random.randint(len(far))]
    return np.exp2(a.ravel()).repeat(32)


def f64(x):
    return np.asarray(x).astype(np.float64)


def striped(idx):
    return np.tile(np.asarray(idx).reshape(-1, 16).T, (8, 1)).astype(np.uint16)


def unstriped(offs):
    return offs[:16].T.reshape(-1).astype(np.int64)


E2M1 = np.array([0.0, 0.5, 1.0, 1.5, 2.0, 3.0, 4.0, 6.0, -0.0, -0.5, -1.0, -1.5, -2.0, -3.0, -4.0, -6.0])


def pack_weight(w, fmt):
    k, n = w.shape
    w = f64(np.asarray(w, np.float32).astype(ml_dtypes.bfloat16)).reshape(k // 32, 32, n)
    amax = np.abs(w).max(1)
    if fmt in ("e4m3", "e5m2"):
        byte = np.frexp(amax)[1] - 1 + 127 - (7 if fmt == "e4m3" else 14)
    else:
        mant, ex = np.frexp(amax / 6.0)
        byte = np.where(mant > 0.5, ex, ex - 1) + 127
    byte = np.clip(np.where(amax > 0, byte, 1), 1, 254)
    scaled = (w * np.exp2(127.0 - byte)[:, None, :]).reshape(k, n).astype(np.float32)
    by_word = np.ascontiguousarray(scaled.reshape(k // 512, 128, 4, n).transpose(0, 1, 3, 2))
    if fmt in ("e4m3", "e5m2"):
        words = by_word.astype(ml_dtypes.float8_e4m3fn if fmt == "e4m3" else ml_dtypes.float8_e5m2).view(np.uint8)
    else:
        c = by_word.astype(ml_dtypes.float4_e2m1fn).view(np.uint8) & 0xF
        words = (c[..., 0::2] | (c[..., 1::2] << 4)).reshape(k // 512, 128, 2 * n)
    return np.ascontiguousarray(words), np.ascontiguousarray(byte.astype(np.uint8).reshape(k // 512, 16, n))


def unpack_weight(words, scales, fmt):
    g, _, n = scales.shape
    words = np.ascontiguousarray(words).reshape(g, 128, n, -1)
    if fmt in ("e4m3", "e5m2"):
        vals = words.view(ml_dtypes.float8_e4m3fn if fmt == "e4m3" else ml_dtypes.float8_e5m2).astype(np.float64)
    else:
        nib = np.empty((g, 128, n, 4), np.uint8)
        nib[..., 0::2] = words & 0xF
        nib[..., 1::2] = words >> 4
        vals = E2M1[nib]
    vals = vals * np.repeat(np.exp2(scales.astype(np.float64) - 127.0), 8, axis=1)[..., None]
    return vals.transpose(0, 1, 3, 2).reshape(g * 512, n)


def bf(x):
    return np.asarray(x, np.float32).astype(ml_dtypes.bfloat16)


def planes(Y):
    r, m = Y.shape
    b = f64(bf(Y)).reshape(r // 32, 32, m)
    amax = np.abs(b).max(1)
    byte = np.clip(np.where(amax > 0, np.frexp(amax)[1] - 1 + 127 - 7, 1), 1, 254)
    codes = (b * np.exp2(127.0 - byte)[:, None, :]).reshape(r, m).astype(np.float32).astype(ml_dtypes.float8_e4m3fn).view(np.uint8)
    words = codes.reshape(r // 512, 128, 4, m).transpose(0, 1, 3, 2)
    return np.ascontiguousarray(words), np.ascontiguousarray(byte.astype(np.uint8).reshape(r // 512, 16, m))


K, T, J, R, N = 1024, 1024, 384, 512, 512


def setup_inputs():
    n = np.random.standard_normal
    idx = np.random.permutation(T)[:J]
    idx2 = np.random.permutation(T)[:J]
    fk = mx_kscale(K)
    fr = mx_kscale(R)
    wp = pack_weight(n((K, R)) * 1 / np.sqrt(K) * fk[:, None] * fr, "e5m2")
    wbp = pack_weight(n((R, N)) * 1 / np.sqrt(R) / fr[:, None], "e2m1")
    return {
        "xf": (n((K, T))).astype(np.float32),
        "fk": (np.random.uniform(0.5, 2.0, (K, 1)) / fk[:, None]).astype(np.float32),
        "w_words": wp[0],
        "w_scales": wp[1],
        "wb_words": wbp[0],
        "wb_scales": wbp[1],
        "hi": (np.random.uniform(0.4, 1.2, (N, 1))).astype(np.float32),
        "rw": (np.random.uniform(0.5, 2.0, (1, J))).astype(np.float32),
        "offs": striped(idx),
        "offs2": striped(idx2),
    }


def reference(xf, fk, w_words, w_scales, wb_words, wb_scales, hi, rw, offs, offs2):
    idx = unstriped(offs)
    idx2 = unstriped(offs2)
    wu = unpack_weight(w_words, w_scales, "e5m2")
    wbu = unpack_weight(wb_words, wb_scales, "e2m1")
    u = (f64(xf)[:, idx] - f64(xf)[:, idx2]) * f64(fk)
    uq = mxq(u, 0, "e4m3")
    a = wu.T @ uq
    pk1 = np.max(a, axis=1, keepdims=True)
    hid = np.maximum(a - 0.4 * pk1, 0.0)
    hidq = mxq(hid, 0, "e4m3")
    p = wbu.T @ hidq
    y = np.minimum(p - f64(hi), 0.0) * f64(rw)
    words, scales = planes(y)
    return y, words, scales

@@ -1,0 +1,238 @@
+from contextlib import ExitStack
+
+import concourse.mybir as mybir
+
+K, T, J, R, N = 1024, 1024, 384, 512, 512
+FLOPS = 2 * K * R * J + 2 * R * N * J
+
+F32 = mybir.dt.float32
+BF16 = mybir.dt.bfloat16
+I32 = mybir.dt.int32
+U32 = mybir.dt.uint32
+U16 = mybir.dt.uint16
+U8 = mybir.dt.uint8
+E4M3 = mybir.dt.float8_e4m3fn_x4
+E5M2 = mybir.dt.float8_e5m2_x4
+E2M1 = mybir.dt.float4_e2m1fn_x4
+ALU = mybir.AluOpType
+ACT = mybir.ActivationFunctionType
+
+P = 128
+PACK = 4
+PASSES = K // (P * PACK)
+CHUNKS = ((0, 128), (128, 256), (256, 384))
+WIDE = ((0, 256), (256, 384))
+BOTH_ON_SCALAR = (5,)
+BOTH_APART = (0,)
+PEAK_SHARE = 0.4
+
+
+def tile_list_pickgaps_peakgated_capped_pl_kernel(
+    tc, xf, fk, w_words, w_scales, wb_words, wb_scales, hi, rw, offs, offs2, out_0, out_1, out_2
+):
+    nc = tc.nc
+    with ExitStack() as ctx:
+        keep = ctx.enter_context(tc.tile_pool(name="keep", bufs=1))
+        psum = ctx.enter_context(tc.psum_pool(name="psum", bufs=1))
+
+        def sb(name, shape, dtype, tag=""):
+            return keep.tile(shape, dtype, name=name, tag=tag or name, align_bytes=64)
+
+        first = sb("first", [P, J // 16], U16)
+        second = sb("second", [P, J // 16], U16)
+        hi_sb = sb("hi_sb", [P, PACK], F32)
+        nc.scalar.dma_start(hi_sb[:], hi.rearrange("(p t) o -> p (t o)", t=PACK))
+        neg_hi = sb("neg_hi", [P, PACK], F32)
+        nc.scalar.activation(neg_hi[:], hi_sb[:], ACT.Copy, scale=-1.0)
+
+        x = [sb("x%d" % i, [P, T], F32) for i in range(PASSES * PACK)]
+        x_rows = xf.rearrange("(a p t) c -> a t p c", a=PASSES, t=PACK)
+
+        def load_x(i):
+            nc.sync.dma_start(x[i][:], x_rows[i // PACK, i % PACK])
+
+        w_sc_raw = sb("w_sc_raw", [P, PASSES, R], U8)
+        wb_sc_raw = sb("wb_sc_raw", [P, 1, N], U8)
+        nc.gpsimd.memset(w_sc_raw[:].bitcast(I32), 0)
+        nc.gpsimd.memset(wb_sc_raw[:].bitcast(I32), 0)
+
+        def load_scales(raw, src):
+            for q in range(4):
+                nc.sync.dma_start(
+                    raw[32 * q : 32 * q + 4].bitcast(I32),
+                    src[:, 4 * q : 4 * q + 4, :].rearrange("z r c -> r z c").bitcast(I32),
+                )
+
+        w_raw = [sb("w_raw%d" % a, [P, R], U32) for a in range(PASSES)]
+
+        def load_w(a):
+            nc.sync.dma_start(w_raw[a][:].bitcast(I32), w_words[a].rearrange("p c t -> p (c t)").bitcast(I32))
+
+        fk_sb = sb("fk_sb", [P, PASSES, PACK], F32)
+        rw_sb = sb("rw_sb", [P, J], F32)
+        wb_raw = sb("wb_raw", [P, N], U16)
+
+        nc.sync.dma_start(second[:], offs2)
+        load_x(0)
+        nc.sync.dma_start(first[:], offs)
+        load_x(1)
+        load_scales(w_sc_raw, w_scales)
+        load_x(2)
+        load_x(3)
+        load_x(4)
+        nc.sync.dma_start(fk_sb[:], fk.rearrange("(a p t) o -> p a (t o)", a=PASSES, t=PACK))
+        load_x(5)
+        load_x(6)
+        load_x(7)
+        load_w(0)
+        load_w(1)
+        load_scales(wb_sc_raw, wb_scales)
+        nc.sync.dma_start(wb_raw[:].bitcast(I32), wb_words[0].bitcast(I32))
+        nc.sync.dma_start(rw_sb[:], rw[0].partition_broadcast(P))
+
+        w_sc = sb("w_sc", [P, PASSES, PACK, P], U8)
+        nc.vector.tensor_copy(w_sc[:], w_sc_raw[:].rearrange("p a (m t) -> p a t m", t=PACK))
+
+        w_dealt = [sb("w_dealt%d" % a, [P, PACK, P], U32) for a in range(PASSES)]
+
+        def deal_w(a):
+            nc.scalar.copy(w_dealt[a][:].rearrange("p t m -> p m t"), w_raw[a][:].rearrange("p (m t) -> p m t", t=PACK))
+
+        def quantise(name, grouped, width):
+            codes = sb(name + "_codes", [P, width], U32)
+            scales = sb(name + "_scales", [P, width], U8)
+            nc.vector.quantize_mx(
+                out=codes[:].bitcast(E4M3), scales=scales[:], in_=grouped[:].rearrange("p j t -> p (j t)")
+            )
+            return codes, scales
+
+        a_ps = [psum.tile([P, J], F32, name="a_ps%d" % t) for t in range(PACK)]
+        gaps = [sb("gaps%d" % a, [P, PACK, J], F32) for a in range(PASSES)]
+
+        def gather(i):
+            gap = gaps[i // PACK][:, i % PACK, :]
+            taken = sb("taken%d" % i, [P, J], F32)
+            nc.scalar.activation(taken[:], x[i][:].indirect(second[:]), ACT.Copy)
+            if i in BOTH_ON_SCALAR or i in BOTH_APART:
+                kept = sb("kept%d" % i, [P, J], F32)
+                if i in BOTH_ON_SCALAR:
+                    nc.scalar.activation(kept[:], x[i][:].indirect(first[:]), ACT.Copy)
+                else:
+                    nc.vector.tensor_copy(kept[:], x[i][:].indirect(first[:]))
+                nc.vector.tensor_tensor(gap, kept[:], taken[:], ALU.subtract)
+            else:
+                nc.vector.tensor_tensor(gap, x[i][:].indirect(first[:]), taken[:], ALU.subtract)
+
+        def scale_and_group(a, lo, hi_col):
+            width = hi_col - lo
+            grouped = sb("u%d_%d" % (a, lo), [P, width, PACK], BF16)
+            nc.vector.tensor_tensor(
+                grouped[:].rearrange("p (c i) t -> p c t i", i=2),
+                gaps[a][:, :, lo:hi_col].rearrange("p t (c i) -> p c t i", i=2),
+                fk_sb[:, a, :].unsqueeze(1).unsqueeze(3).to_broadcast([P, width // 2, PACK, 2]),
+                ALU.mult,
+            )
+            return grouped
+
+        def first_product(a, lo, up, codes, scales):
+            for t in range(PACK):
+                nc.tensor.matmul_mx(
+                    out=a_ps[t][:, lo:up],
+                    lhsT=w_dealt[a][:, t, :].bitcast(E5M2),
+                    lhsT_scale=w_sc[:, a, t, :],
+                    rhs=codes.bitcast(E4M3),
+                    rhs_scale=scales,
+                    start=(a == 0 and lo == 0),
+                    stop=(a == PASSES - 1 and up == J),
+                )
+
+        def group(name, planar, width, on_scalar):
+            grouped = sb(name, [P, width, PACK], BF16)
+            dst = grouped[:].rearrange("p (c i) t -> p c t i", i=4)
+            src = planar.rearrange("p t (c i) -> p c t i", i=4)
+            if on_scalar:
+                nc.scalar.copy(dst, src)
+            else:
+                nc.vector.tensor_copy(dst, src)
+            return grouped
+
+        for i in range(PACK):
+            gather(i)
+        grouped = scale_and_group(0, 0, J)
+        gather(PACK)
+        codes, scales = quantise("u0", grouped, J)
+        for i in range(PACK + 1, 2 * PACK):
+            gather(i)
+        deal_w(0)
+        for lo, up in WIDE:
+            first_product(0, lo, up, codes[:, lo:up], scales[:, lo:up])
+        deal_w(1)
+        groups = [scale_and_group(1, lo, up) for lo, up in CHUNKS[:-1]]
+        lo, up = CHUNKS[-1]
+        last = sb("u1_last", [P, PACK, up - lo], BF16, tag="taken7")
+        for t in range(PACK):
+            nc.scalar.activation(last[:, t, :], gaps[1][:, t, lo:up], ACT.Copy, scale=fk_sb[:, 1, t : t + 1])
+        groups.append(group("u1_last_grouped", last[:], up - lo, True))
+        for c, (lo, up) in enumerate(CHUNKS):
+            codes, scales = quantise("u1_%d" % c, groups[c], up - lo)
+            first_product(1, lo, up, codes[:], scales[:])
+
+        wb_sc = sb("wb_sc", [P, PACK, P], U8)
+        nc.vector.tensor_copy(wb_sc[:], wb_sc_raw[:, 0, :].rearrange("p (m t) -> p t m", t=PACK))
+        wb_dealt = sb("wb_dealt", [P, PACK, P], U16)
+        nc.scalar.copy(wb_dealt[:], wb_raw[:].rearrange("p (m t) -> p t m", t=PACK))
+
+        neg_bar = sb("neg_bar", [P, PACK], F32)
+        unread = sb("unread", [P, J], BF16)
+        hid = sb("hid", [P, PACK, J], BF16)
+        for t in range(PACK):
+            nc.vector.tensor_scalar(
+                unread[:], a_ps[t][:], -PEAK_SHARE, None, ALU.mult, ALU.min, accum_out=neg_bar[:, t : t + 1]
+            )
+            nc.scalar.activation(hid[:, t, :], a_ps[t][:], ACT.Relu, bias=neg_bar[:, t : t + 1])
+
+        n_chunks = len(CHUNKS)
+        p_ps = [psum.tile([P, PACK, P], F32, name="p_ps%d" % c) for c in range(n_chunks)]
+        groups = [
+            group("hid%d" % c, hid[:, :, lo:up], up - lo, c == n_chunks - 1) for c, (lo, up) in enumerate(CHUNKS)
+        ]
+        for c, (lo, up) in enumerate(CHUNKS):
+            codes, scales = quantise("h%d" % c, groups[c], up - lo)
+            for t in range(PACK):
+                nc.tensor.matmul_mx(
+                    out=p_ps[c][:, t, :],
+                    lhsT=wb_dealt[:, t, :].bitcast(E2M1),
+                    lhsT_scale=wb_sc[:, t, :],
+                    rhs=codes[:].bitcast(E4M3),
+                    rhs_scale=scales[:],
+                    start=True,
+                    stop=True,
+                )
+
+        y_rows = out_0.rearrange("(p t) j -> p t j", t=PACK)
+        y_codes = sb("y_codes", [P, J], U32)
+        y_scales = sb("y_scales", [P, J], U8)
+        ys = []
+        for c, (lo, up) in enumerate(CHUNKS):
+            below = sb("below%d" % c, [P, PACK, P], F32)
+            for t in range(PACK):
+                nc.scalar.activation(below[:, t, :], p_ps[c][:, t, :], ACT.Identity, bias=neg_hi[:, t : t + 1])
+            y = sb("y%d" % c, [P, PACK, P], F32)
+            nc.vector.scalar_tensor_tensor(
+                y[:], below[:], 0.0, rw_sb[:, lo:up].unsqueeze(1).to_broadcast([P, PACK, P]), ALU.min, ALU.mult
+            )
+            nc.sync.dma_start(y_rows[:, :, lo:up], y[:])
+            ys.append(y)
+        groups = [group("y_grouped%d" % c, ys[c][:], P, c == 1) for c in range(n_chunks)]
+        for c, (lo, up) in enumerate(CHUNKS):
+            nc.vector.quantize_mx(
+                out=y_codes[:, lo:up].bitcast(E4M3),
+                scales=y_scales[:, lo:up],
+                in_=groups[c][:].rearrange("p j t -> p (j t)"),
+            )
+        nc.sync.dma_start(out_1[0].rearrange("p j t -> p (j t)").bitcast(I32), y_codes[:].bitcast(I32))
+        for q in range(4):
+            queue = nc.scalar if q % 2 == 0 else nc.sync
+            queue.dma_start(
+                out_2[0, 4 * q : 4 * q + 4, :].bitcast(I32), y_scales[32 * q : 32 * q + 4, :].bitcast(I32)
+            )

@@ -106,7 +106,7 @@ def tile_list_pickgaps_peakgated_capped_pl_kernel(
             )
             return codes, scales
 
-        a_ps = [psum.tile([P, J], F32, name="a_ps%d" % t) for t in range(PACK)]
+        a_ps = [psum.tile([P, J], F32, name="a_ps%d" % t, tag="bank%d" % t) for t in range(PACK)]
         gaps = [sb("gaps%d" % a, [P, PACK, J], F32) for a in range(PASSES)]
 
         def gather(i):
@@ -169,7 +169,7 @@ def tile_list_pickgaps_peakgated_capped_pl_kernel(
         deal_w(1)
         groups = [scale_and_group(1, lo, up) for lo, up in CHUNKS[:-1]]
         lo, up = CHUNKS[-1]
-        last = sb("u1_last", [P, PACK, up - lo], BF16, tag="taken7")
+        last = sb("u1_last", [P, PACK, up - lo], BF16, tag="w_raw1")
         for t in range(PACK):
             nc.scalar.activation(last[:, t, :], gaps[1][:, t, lo:up], ACT.Copy, scale=fk_sb[:, 1, t : t + 1])
         groups.append(group("u1_last_grouped", last[:], up - lo, True))
@@ -183,16 +183,27 @@ def tile_list_pickgaps_peakgated_capped_pl_kernel(
         nc.scalar.copy(wb_dealt[:], wb_raw[:].rearrange("p (m t) -> p t m", t=PACK))
 
         neg_bar = sb("neg_bar", [P, PACK], F32)
-        unread = sb("unread", [P, J], BF16)
         hid = sb("hid", [P, PACK, J], BF16)
         for t in range(PACK):
+            unread = sb("unread%d" % t, [P, J], BF16)
             nc.vector.tensor_scalar(
                 unread[:], a_ps[t][:], -PEAK_SHARE, None, ALU.mult, ALU.min, accum_out=neg_bar[:, t : t + 1]
             )
-            nc.scalar.activation(hid[:, t, :], a_ps[t][:], ACT.Relu, bias=neg_bar[:, t : t + 1])
+            split = P if t == PACK - 1 else 0
+            if split:
+                nc.vector.tensor_scalar(
+                    hid[:, t, :split], a_ps[t][:, :split], neg_bar[:, t : t + 1], 0.0, ALU.add, ALU.max
+                )
+            nc.scalar.activation(hid[:, t, split:], a_ps[t][:, split:], ACT.Relu, bias=neg_bar[:, t : t + 1])
 
         n_chunks = len(CHUNKS)
-        p_ps = [psum.tile([P, PACK, P], F32, name="p_ps%d" % c) for c in range(n_chunks)]
+        p_banks = [
+            psum.tile([P, 2, P], F32, name="p_ps%d" % b, tag="bank%d" % ((PACK + b) % 8)) for b in range(2 * n_chunks)
+        ]
+
+        def p_ps(c, t):
+            return p_banks[2 * c + t // 2][:, t % 2, :]
+
         groups = [
             group("hid%d" % c, hid[:, :, lo:up], up - lo, c == n_chunks - 1) for c, (lo, up) in enumerate(CHUNKS)
         ]
@@ -200,7 +211,7 @@ def tile_list_pickgaps_peakgated_capped_pl_kernel(
             codes, scales = quantise("h%d" % c, groups[c], up - lo)
             for t in range(PACK):
                 nc.tensor.matmul_mx(
-                    out=p_ps[c][:, t, :],
+                    out=p_ps(c, t),
                     lhsT=wb_dealt[:, t, :].bitcast(E2M1),
                     lhsT_scale=wb_sc[:, t, :],
                     rhs=codes[:].bitcast(E4M3),
@@ -216,21 +227,33 @@ def tile_list_pickgaps_peakgated_capped_pl_kernel(
         for c, (lo, up) in enumerate(CHUNKS):
             below = sb("below%d" % c, [P, PACK, P], F32)
             for t in range(PACK):
-                nc.scalar.activation(below[:, t, :], p_ps[c][:, t, :], ACT.Identity, bias=neg_hi[:, t : t + 1])
+                if c == 0 and t >= 2:
+                    nc.vector.tensor_scalar(below[:, t, :], p_ps(c, t), neg_hi[:, t : t + 1], None, ALU.add)
+                else:
+                    nc.scalar.activation(below[:, t, :], p_ps(c, t), ACT.Identity, bias=neg_hi[:, t : t + 1])
             y = sb("y%d" % c, [P, PACK, P], F32)
-            nc.vector.scalar_tensor_tensor(
-                y[:], below[:], 0.0, rw_sb[:, lo:up].unsqueeze(1).to_broadcast([P, PACK, P]), ALU.min, ALU.mult
-            )
+            step = 2 if c == n_chunks - 1 else PACK
+            for t in range(0, PACK, step):
+                nc.vector.scalar_tensor_tensor(
+                    y[:, t : t + step, :],
+                    below[:, t : t + step, :],
+                    0.0,
+                    rw_sb[:, lo:up].unsqueeze(1).to_broadcast([P, step, P]),
+                    ALU.min,
+                    ALU.mult,
+                )
             nc.sync.dma_start(y_rows[:, :, lo:up], y[:])
             ys.append(y)
-        groups = [group("y_grouped%d" % c, ys[c][:], P, c == 1) for c in range(n_chunks)]
+        groups = [group("y_grouped%d" % c, ys[c][:], P, c in (0, 1)) for c in range(n_chunks)]
         for c, (lo, up) in enumerate(CHUNKS):
             nc.vector.quantize_mx(
                 out=y_codes[:, lo:up].bitcast(E4M3),
                 scales=y_scales[:, lo:up],
                 in_=groups[c][:].rearrange("p j t -> p (j t)"),
             )
-        nc.sync.dma_start(out_1[0].rearrange("p j t -> p (j t)").bitcast(I32), y_codes[:].bitcast(I32))
+        word_rows = out_1[0].rearrange("p j t -> p (j t)").bitcast(I32)
+        for lo, up in WIDE:
+            nc.sync.dma_start(word_rows[:, lo:up], y_codes[:, lo:up].bitcast(I32))
         for q in range(4):
             queue = nc.scalar if q % 2 == 0 else nc.sync
             queue.dma_start(

from contextlib import ExitStack

import concourse.mybir as mybir

K, T, J, R, N = 1024, 1024, 384, 512, 512
FLOPS = 2 * K * R * J + 2 * R * N * J

F32 = mybir.dt.float32
BF16 = mybir.dt.bfloat16
I32 = mybir.dt.int32
U32 = mybir.dt.uint32
U16 = mybir.dt.uint16
U8 = mybir.dt.uint8
E4M3 = mybir.dt.float8_e4m3fn_x4
E5M2 = mybir.dt.float8_e5m2_x4
E2M1 = mybir.dt.float4_e2m1fn_x4
ALU = mybir.AluOpType
ACT = mybir.ActivationFunctionType

P = 128
PACK = 4
PASSES = K // (P * PACK)
CHUNKS = ((0, 128), (128, 256), (256, 384))
WIDE = ((0, 256), (256, 384))
BOTH_ON_SCALAR = (5,)
BOTH_APART = (0,)
PEAK_SHARE = 0.4


def tile_list_pickgaps_peakgated_capped_pl_kernel(
    tc, xf, fk, w_words, w_scales, wb_words, wb_scales, hi, rw, offs, offs2, out_0, out_1, out_2
):
    nc = tc.nc
    with ExitStack() as ctx:
        keep = ctx.enter_context(tc.tile_pool(name="keep", bufs=1))
        psum = ctx.enter_context(tc.psum_pool(name="psum", bufs=1))

        def sb(name, shape, dtype, tag=""):
            return keep.tile(shape, dtype, name=name, tag=tag or name, align_bytes=64)

        first = sb("first", [P, J // 16], U16)
        second = sb("second", [P, J // 16], U16)
        hi_sb = sb("hi_sb", [P, PACK], F32)
        nc.scalar.dma_start(hi_sb[:], hi.rearrange("(p t) o -> p (t o)", t=PACK))
        neg_hi = sb("neg_hi", [P, PACK], F32)
        nc.scalar.activation(neg_hi[:], hi_sb[:], ACT.Copy, scale=-1.0)

        x = [sb("x%d" % i, [P, T], F32) for i in range(PASSES * PACK)]
        x_rows = xf.rearrange("(a p t) c -> a t p c", a=PASSES, t=PACK)

        def load_x(i):
            nc.sync.dma_start(x[i][:], x_rows[i // PACK, i % PACK])

        w_sc_raw = sb("w_sc_raw", [P, PASSES, R], U8)
        wb_sc_raw = sb("wb_sc_raw", [P, 1, N], U8)
        nc.gpsimd.memset(w_sc_raw[:].bitcast(I32), 0)
        nc.gpsimd.memset(wb_sc_raw[:].bitcast(I32), 0)

        def load_scales(raw, src):
            for q in range(4):
                nc.sync.dma_start(
                    raw[32 * q : 32 * q + 4].bitcast(I32),
                    src[:, 4 * q : 4 * q + 4, :].rearrange("z r c -> r z c").bitcast(I32),
                )

        w_raw = [sb("w_raw%d" % a, [P, R], U32) for a in range(PASSES)]

        def load_w(a):
            nc.sync.dma_start(w_raw[a][:].bitcast(I32), w_words[a].rearrange("p c t -> p (c t)").bitcast(I32))

        fk_sb = sb("fk_sb", [P, PASSES, PACK], F32)
        rw_sb = sb("rw_sb", [P, J], F32)
        wb_raw = sb("wb_raw", [P, N], U16)

        nc.sync.dma_start(second[:], offs2)
        load_x(0)
        nc.sync.dma_start(first[:], offs)
        load_x(1)
        load_scales(w_sc_raw, w_scales)
        load_x(2)
        load_x(3)
        load_x(4)
        nc.sync.dma_start(fk_sb[:], fk.rearrange("(a p t) o -> p a (t o)", a=PASSES, t=PACK))
        load_x(5)
        load_x(6)
        load_x(7)
        load_w(0)
        load_w(1)
        load_scales(wb_sc_raw, wb_scales)
        nc.sync.dma_start(wb_raw[:].bitcast(I32), wb_words[0].bitcast(I32))
        nc.sync.dma_start(rw_sb[:], rw[0].partition_broadcast(P))

        w_sc = sb("w_sc", [P, PASSES, PACK, P], U8)
        nc.vector.tensor_copy(w_sc[:], w_sc_raw[:].rearrange("p a (m t) -> p a t m", t=PACK))

        w_dealt = [sb("w_dealt%d" % a, [P, PACK, P], U32) for a in range(PASSES)]

        def deal_w(a):
            nc.scalar.copy(w_dealt[a][:].rearrange("p t m -> p m t"), w_raw[a][:].rearrange("p (m t) -> p m t", t=PACK))

        def quantise(name, grouped, width):
            codes = sb(name + "_codes", [P, width], U32)
            scales = sb(name + "_scales", [P, width], U8)
            nc.vector.quantize_mx(
                out=codes[:].bitcast(E4M3), scales=scales[:], in_=grouped[:].rearrange("p j t -> p (j t)")
            )
            return codes, scales

        a_ps = [psum.tile([P, J], F32, name="a_ps%d" % t, tag="bank%d" % t) for t in range(PACK)]
        gaps = [sb("gaps%d" % a, [P, PACK, J], F32) for a in range(PASSES)]

        def gather(i):
            gap = gaps[i // PACK][:, i % PACK, :]
            taken = sb("taken%d" % i, [P, J], F32)
            nc.scalar.activation(taken[:], x[i][:].indirect(second[:]), ACT.Copy)
            if i in BOTH_ON_SCALAR or i in BOTH_APART:
                kept = sb("kept%d" % i, [P, J], F32)
                if i in BOTH_ON_SCALAR:
                    nc.scalar.activation(kept[:], x[i][:].indirect(first[:]), ACT.Copy)
                else:
                    nc.vector.tensor_copy(kept[:], x[i][:].indirect(first[:]))
                nc.vector.tensor_tensor(gap, kept[:], taken[:], ALU.subtract)
            else:
                nc.vector.tensor_tensor(gap, x[i][:].indirect(first[:]), taken[:], ALU.subtract)

        def scale_and_group(a, lo, hi_col):
            width = hi_col - lo
            grouped = sb("u%d_%d" % (a, lo), [P, width, PACK], BF16)
            nc.vector.tensor_tensor(
                grouped[:].rearrange("p (c i) t -> p c t i", i=2),
                gaps[a][:, :, lo:hi_col].rearrange("p t (c i) -> p c t i", i=2),
                fk_sb[:, a, :].unsqueeze(1).unsqueeze(3).to_broadcast([P, width // 2, PACK, 2]),
                ALU.mult,
            )
            return grouped

        def first_product(a, lo, up, codes, scales):
            for t in range(PACK):
                nc.tensor.matmul_mx(
                    out=a_ps[t][:, lo:up],
                    lhsT=w_dealt[a][:, t, :].bitcast(E5M2),
                    lhsT_scale=w_sc[:, a, t, :],
                    rhs=codes.bitcast(E4M3),
                    rhs_scale=scales,
                    start=(a == 0 and lo == 0),
                    stop=(a == PASSES - 1 and up == J),
                )

        def group(name, planar, width, on_scalar):
            grouped = sb(name, [P, width, PACK], BF16)
            dst = grouped[:].rearrange("p (c i) t -> p c t i", i=4)
            src = planar.rearrange("p t (c i) -> p c t i", i=4)
            if on_scalar:
                nc.scalar.copy(dst, src)
            else:
                nc.vector.tensor_copy(dst, src)
            return grouped

        for i in range(PACK):
            gather(i)
        grouped = scale_and_group(0, 0, J)
        gather(PACK)
        codes, scales = quantise("u0", grouped, J)
        for i in range(PACK + 1, 2 * PACK):
            gather(i)
        deal_w(0)
        for lo, up in WIDE:
            first_product(0, lo, up, codes[:, lo:up], scales[:, lo:up])
        deal_w(1)
        groups = [scale_and_group(1, lo, up) for lo, up in CHUNKS[:-1]]
        lo, up = CHUNKS[-1]
        last = sb("u1_last", [P, PACK, up - lo], BF16, tag="w_raw1")
        for t in range(PACK):
            nc.scalar.activation(last[:, t, :], gaps[1][:, t, lo:up], ACT.Copy, scale=fk_sb[:, 1, t : t + 1])
        groups.append(group("u1_last_grouped", last[:], up - lo, True))
        for c, (lo, up) in enumerate(CHUNKS):
            codes, scales = quantise("u1_%d" % c, groups[c], up - lo)
            first_product(1, lo, up, codes[:], scales[:])

        wb_sc = sb("wb_sc", [P, PACK, P], U8)
        nc.vector.tensor_copy(wb_sc[:], wb_sc_raw[:, 0, :].rearrange("p (m t) -> p t m", t=PACK))
        wb_dealt = sb("wb_dealt", [P, PACK, P], U16)
        nc.scalar.copy(wb_dealt[:], wb_raw[:].rearrange("p (m t) -> p t m", t=PACK))

        neg_bar = sb("neg_bar", [P, PACK], F32)
        hid = sb("hid", [P, PACK, J], BF16)
        for t in range(PACK):
            unread = sb("unread%d" % t, [P, J], BF16)
            nc.vector.tensor_scalar(
                unread[:], a_ps[t][:], -PEAK_SHARE, None, ALU.mult, ALU.min, accum_out=neg_bar[:, t : t + 1]
            )
            split = P if t == PACK - 1 else 0
            if split:
                nc.vector.tensor_scalar(
                    hid[:, t, :split], a_ps[t][:, :split], neg_bar[:, t : t + 1], 0.0, ALU.add, ALU.max
                )
            nc.scalar.activation(hid[:, t, split:], a_ps[t][:, split:], ACT.Relu, bias=neg_bar[:, t : t + 1])

        n_chunks = len(CHUNKS)
        p_banks = [
            psum.tile([P, 2, P], F32, name="p_ps%d" % b, tag="bank%d" % ((PACK + b) % 8)) for b in range(2 * n_chunks)
        ]

        def p_ps(c, t):
            return p_banks[2 * c + t // 2][:, t % 2, :]

        groups = [
            group("hid%d" % c, hid[:, :, lo:up], up - lo, c == n_chunks - 1) for c, (lo, up) in enumerate(CHUNKS)
        ]
        for c, (lo, up) in enumerate(CHUNKS):
            codes, scales = quantise("h%d" % c, groups[c], up - lo)
            for t in range(PACK):
                nc.tensor.matmul_mx(
                    out=p_ps(c, t),
                    lhsT=wb_dealt[:, t, :].bitcast(E2M1),
                    lhsT_scale=wb_sc[:, t, :],
                    rhs=codes[:].bitcast(E4M3),
                    rhs_scale=scales[:],
                    start=True,
                    stop=True,
                )

        y_rows = out_0.rearrange("(p t) j -> p t j", t=PACK)
        y_codes = sb("y_codes", [P, J], U32)
        y_scales = sb("y_scales", [P, J], U8)
        ys = []
        for c, (lo, up) in enumerate(CHUNKS):
            below = sb("below%d" % c, [P, PACK, P], F32)
            for t in range(PACK):
                if c == 0 and t >= 2:
                    nc.vector.tensor_scalar(below[:, t, :], p_ps(c, t), neg_hi[:, t : t + 1], None, ALU.add)
                else:
                    nc.scalar.activation(below[:, t, :], p_ps(c, t), ACT.Identity, bias=neg_hi[:, t : t + 1])
            y = sb("y%d" % c, [P, PACK, P], F32)
            step = 2 if c == n_chunks - 1 else PACK
            for t in range(0, PACK, step):
                nc.vector.scalar_tensor_tensor(
                    y[:, t : t + step, :],
                    below[:, t : t + step, :],
                    0.0,
                    rw_sb[:, lo:up].unsqueeze(1).to_broadcast([P, step, P]),
                    ALU.min,
                    ALU.mult,
                )
            nc.sync.dma_start(y_rows[:, :, lo:up], y[:])
            ys.append(y)
        groups = [group("y_grouped%d" % c, ys[c][:], P, c in (0, 1)) for c in range(n_chunks)]
        for c, (lo, up) in enumerate(CHUNKS):
            nc.vector.quantize_mx(
                out=y_codes[:, lo:up].bitcast(E4M3),
                scales=y_scales[:, lo:up],
                in_=groups[c][:].rearrange("p j t -> p (j t)"),
            )
        word_rows = out_1[0].rearrange("p j t -> p (j t)").bitcast(I32)
        for lo, up in WIDE:
            nc.sync.dma_start(word_rows[:, lo:up], y_codes[:, lo:up].bitcast(I32))
        for q in range(4):
            queue = nc.scalar if q % 2 == 0 else nc.sync
            queue.dma_start(
                out_2[0, 4 * q : 4 * q + 4, :].bitcast(I32), y_scales[32 * q : 32 * q + 4, :].bitcast(I32)
            )
